import numpy as np
import ml_dtypes


def mxq(x, axis, fmt="e4m3"):
    dtype, down = {"e4m3": (ml_dtypes.float8_e4m3fn, 7), "e5m2": (ml_dtypes.float8_e5m2, 14)}[fmt]
    v = np.moveaxis(np.asarray(x, np.float32).astype(ml_dtypes.bfloat16).astype(np.float64), axis, -1)
    blocks = v.reshape(v.shape[:-1] + (-1, 32))
    amax = np.abs(blocks).max(-1, keepdims=True)
    byte = np.maximum(np.where(amax > 0, np.frexp(amax)[1] - 1 + 127, 0) - down, 1)
    scale = np.exp2(byte - 127.0)
    codes = (blocks / scale).astype(np.float32).astype(dtype).astype(np.float64)
    return np.moveaxis((codes * scale).reshape(v.shape), -1, axis)


WIDE = False


def mx_kscale(k):
    if not WIDE:
        return np.ones(k)
    levels = np.array([10, -10, 5, -5, 0])
    if k % 512:
        return np.exp2(np.random.permutation(np.resize(levels, k // 32))).repeat(32)
    a = np.empty((k // 512, 16))
    for p in range(k // 512):
        a[p, :8] = np.random.permutation(np.resize(levels, 8))
        for g in range(8):
            far = levels[np.abs(levels - a[p, g]) >= 10]
            a[p, g + 8] = far[np.random.randint(len(far))]
    return np.exp2(a.ravel()).repeat(32)


def f64(x):
    return np.asarray(x).astype(np.float64)


def striped(idx):
    return np.tile(np.asarray(idx).reshape(-1, 16).T, (8, 1)).astype(np.uint16)


def unstriped(offs):
    return offs[:16].T.reshape(-1).astype(np.int64)


E2M1 = np.array([0.0, 0.5, 1.0, 1.5, 2.0, 3.0, 4.0, 6.0, -0.0, -0.5, -1.0, -1.5, -2.0, -3.0, -4.0, -6.0])


def pack_weight(w, fmt):
    k, n = w.shape
    w = f64(np.asarray(w, np.float32).astype(ml_dtypes.bfloat16)).reshape(k // 32, 32, n)
    amax = np.abs(w).max(1)
    if fmt == "e4m3":
        byte = np.frexp(amax)[1] - 1 + 127 - 7
    else:
        mant, ex = np.frexp(amax / 6.0)
        byte = np.where(mant > 0.5, ex, ex - 1) + 127
    byte = np.clip(np.where(amax > 0, byte, 1), 1, 254)
    scaled = (w * np.exp2(127.0 - byte)[:, None, :]).reshape(k, n).astype(np.float32)
    by_word = np.ascontiguousarray(scaled.reshape(k // 512, 128, 4, n).transpose(0, 1, 3, 2))
    if fmt == "e4m3":
        words = by_word.astype(ml_dtypes.float8_e4m3fn).view(np.uint8)
    else:
        c = by_word.astype(ml_dtypes.float4_e2m1fn).view(np.uint8) & 0xF
        words = (c[..., 0::2] | (c[..., 1::2] << 4)).reshape(k // 512, 128, 2 * n)
    return np.ascontiguousarray(words), np.ascontiguousarray(byte.astype(np.uint8).reshape(k // 512, 16, n))


def unpack_weight(words, scales, fmt):
    g, _, n = scales.shape
    words = np.ascontiguousarray(words).reshape(g, 128, n, -1)
    if fmt == "e4m3":
        vals = words.view(ml_dtypes.float8_e4m3fn).astype(np.float64)
    else:
        nib = np.empty((g, 128, n, 4), np.uint8)
        nib[..., 0::2] = words & 0xF
        nib[..., 1::2] = words >> 4
        vals = E2M1[nib]
    vals = vals * np.repeat(np.exp2(scales.astype(np.float64) - 127.0), 8, axis=1)[..., None]
    return vals.transpose(0, 1, 3, 2).reshape(g * 512, n)


K, L, T, J, N = 1024, 512, 1024, 512, 512


def setup_inputs():
    n = np.random.standard_normal
    idx = np.random.permutation(T)[:J]
    fk = mx_kscale(K)
    fl = mx_kscale(L)
    xtp = pack_weight(n((K, T)) / fk[:, None], "e4m3")
    wsp = pack_weight(n((K, N)) * 1 / np.sqrt(K) * fk[:, None], "e2m1")
    xep = pack_weight(n((L, J)) / fl[:, None], "e4m3")
    return {
        "xt_words": xtp[0],
        "xt_scales": xtp[1],
        "ws_words": wsp[0],
        "ws_scales": wsp[1],
        "xe_words": xep[0],
        "xe_scales": xep[1],
        "we": (n((L, N)) * 1 / np.sqrt(L) * fl[:, None]).astype(np.float32),
        "res": (1.0 * n((N, T))).astype(np.float32),
        "offs": striped(idx),
    }


def reference(xt_words, xt_scales, ws_words, ws_scales, xe_words, xe_scales, we, res, offs):
    idx = unstriped(offs)
    xtu = unpack_weight(xt_words, xt_scales, "e4m3")
    wsu = unpack_weight(ws_words, ws_scales, "e2m1")
    xeu = unpack_weight(xe_words, xe_scales, "e4m3")
    u = wsu.T @ xtu
    weq = mxq(f64(we), 0, "e4m3")
    p = weq.T @ xeu
    d = np.tanh(p) * u[:, idx]
    dp = np.zeros((N, T))
    dp[:, idx] = d
    y = u - dp + 0.2 * f64(res)
    return y

@@ -1,0 +1,172 @@
+from contextlib import ExitStack
+
+import concourse.mybir as mybir
+
+K, L, T, J, N = 1024, 512, 1024, 512, 512
+FLOPS = 2 * K * N * T + 2 * L * N * J
+
+F32 = mybir.dt.float32
+BF16 = mybir.dt.bfloat16
+I32 = mybir.dt.int32
+U32 = mybir.dt.uint32
+U16 = mybir.dt.uint16
+U8 = mybir.dt.uint8
+FP8X4 = mybir.dt.float8_e4m3fn_x4
+FP4X4 = mybir.dt.float4_e2m1fn_x4
+ACT = mybir.ActivationFunctionType
+ALU = mybir.AluOpType
+
+P = 128
+PACK = 4
+BLOCKS = N // P
+BANK = 512
+PASSES = K // 512
+
+
+def tile_moe_expert_scales_shared_answer_kernel(tc, xt_words, xt_scales, ws_words, ws_scales, xe_words, xe_scales, we, res, offs, out):
+    nc = tc.nc
+    with ExitStack() as ctx:
+        held = ctx.enter_context(tc.tile_pool(name="held", bufs=1))
+        psum_u = ctx.enter_context(tc.psum_pool(name="psum_u", bufs=4))
+        psum_p = ctx.enter_context(tc.psum_pool(name="psum_p", bufs=2))
+
+        def tile(shape, dtype, name, tag=None):
+            return held.tile(shape, dtype, name=name, tag=tag or name, align_bytes=64)
+
+        offsets = held.tile([P, J // 16], U16, name="offsets")
+        xt_plane = tile([P, PASSES, T], U8, "xt_plane")
+        ws_plane = tile([P, PASSES, N], U8, "ws_plane")
+        xe_plane = tile([P, 1, J], U8, "xe_plane")
+
+        def load_plane(queue, plane, scales):
+            rows = scales.rearrange("z (q r) c -> r q z c", r=4)
+            for r in range(4):
+                queue.dma_start(out=plane[r:P:32, :, :].bitcast(I32), in_=rows[r].bitcast(I32))
+
+        we_rows = we.rearrange("(p j) n -> p j n", j=PACK)
+        xt_rows = xt_words.rearrange("z p c r -> p z (c r)")
+
+        def load_tokens(h):
+            half = tile([P, PASSES, BANK], U32, "xt_codes%d" % h)
+            nc.sync.dma_start(out=half[:].bitcast(I32), in_=xt_rows[:, :, 4 * BANK * h : 4 * BANK * (h + 1)].bitcast(I32))
+            return half
+
+        load_plane(nc.sync, xt_plane, xt_scales)
+        we_first = tile([P, PACK, 2 * P], F32, "we_first", tag="window0")
+        nc.sync.dma_start(out=we_first[:], in_=we_rows[:, :, 0 : 2 * P])
+        xe_codes = tile([P, J], U32, "xe_codes")
+        nc.sync.dma_start(out=xe_codes[:].bitcast(I32), in_=xe_words[0].rearrange("p c r -> p (c r)").bitcast(I32))
+        ws_codes = tile([P, PASSES, 2 * N], U8, "ws_codes")
+        nc.sync.dma_start(out=ws_codes[:].bitcast(I32), in_=ws_words.rearrange("z p c -> p z c").bitcast(I32))
+        xt_codes = [load_tokens(0)]
+        load_plane(nc.sync, ws_plane, ws_scales)
+        xt_codes.append(load_tokens(1))
+        load_plane(nc.sync, xe_plane, xe_scales)
+        nc.sync.dma_start(offsets[:], offs)
+
+        we_codes = [None] * BLOCKS
+        we_plane = [None] * BLOCKS
+
+        def interleave(copy, raw, width, name, tag):
+            grouped = tile([P, width, PACK], BF16, name, tag=tag)
+            copy(
+                out=grouped[:].rearrange("p (c i) t -> p c t i", i=4),
+                in_=raw.rearrange("p t (c i) -> p c t i", i=4),
+            )
+            return grouped
+
+        def quantize(grouped, first, count):
+            codes = tile([P, count * P], U32, "we_codes%d" % first)
+            plane = tile([P, count * P], U8, "we_plane%d" % first)
+            nc.vector.quantize_mx(out=codes[:].bitcast(FP8X4), scales=plane[:], in_=grouped[:].rearrange("p w t -> p (w t)"))
+            for i in range(count):
+                we_codes[first + i] = codes[:, i * P : (i + 1) * P]
+                we_plane[first + i] = plane[:, i * P : (i + 1) * P]
+
+        def expert(b):
+            acc = psum_p.tile([P, J], F32, name="p_acc")
+            nc.tensor.matmul_mx(
+                out=acc[:], lhsT=we_codes[b].bitcast(FP8X4), lhsT_scale=we_plane[b],
+                rhs=xe_codes[:].bitcast(FP8X4), rhs_scale=xe_plane[:, 0, :], start=True, stop=True,
+            )
+            gain = tile([P, J], F32, "gain%d" % b, tag="v" if b == 0 else None)
+            nc.scalar.activation(out=gain[:], in_=acc[:], func=ACT.Tanh)
+            return gain
+
+        def shared(b):
+            u = tile([P, T], F32, "u%d" % b)
+            for h in range(2):
+                acc = psum_u.tile([P, BANK], F32, name="u_acc")
+                for z in range(PASSES):
+                    nc.tensor.matmul_mx(
+                        out=acc[:],
+                        lhsT=ws_codes[:, z, 2 * P * b : 2 * P * (b + 1)].bitcast(FP4X4),
+                        lhsT_scale=ws_plane[:, z, P * b : P * (b + 1)],
+                        rhs=xt_codes[h][:, z, :].bitcast(FP8X4),
+                        rhs_scale=xt_plane[:, z, BANK * h : BANK * (h + 1)],
+                        start=(z == 0), stop=(z == PASSES - 1),
+                    )
+                if b == 0 and h == 1:
+                    nc.vector.tensor_copy(out=u[:, BANK * h : BANK * (h + 1)], in_=acc[:])
+                else:
+                    nc.scalar.copy(out=u[:, BANK * h : BANK * (h + 1)], in_=acc[:])
+            return u
+
+        def scaled_residual(b):
+            raw = tile([P, T], F32, "res%d" % b, tag="res_raw")
+            nc.sync.dma_start(out=raw[:], in_=res[P * b : P * (b + 1), :])
+            r = tile([P, T], F32, "r%d" % b, tag="r%d" % b)
+            for h in range(2):
+                cols = slice(BANK * h, BANK * (h + 1))
+                nc.scalar.activation(out=r[:, cols], in_=raw[:, cols], func=ACT.Copy, scale=0.2)
+            return r
+
+        def gather(b, u, gain):
+            d = tile([P, J], F32, "d%d" % b, tag="r%d" % (b - 1) if b else None)
+            nc.vector.tensor_tensor(out=d[:], in0=u[:].indirect(offsets[:]), in1=gain[:], op=ALU.mult)
+            return d
+
+        def scatter(b, d):
+            nc.vector.tensor_copy(out=windows[b % 2][:].indirect(offsets[:]), in_=d[:])
+
+        def plain_sum(b, u, r):
+            v = tile([P, T], F32, "v%d" % b, tag="v")
+            for h in range(2):
+                cols = slice(BANK * h, BANK * (h + 1))
+                nc.gpsimd.tensor_tensor(out=v[:, cols], in0=u[:, cols], in1=r[:, cols], op=ALU.add)
+            return v
+
+        def finish(b, v):
+            pieces = 2 if b == BLOCKS - 1 else 1
+            width = T // pieces
+            for i in range(pieces):
+                cols = slice(width * i, width * (i + 1))
+                y = tile([P, width], F32, "y%d_%d" % (b, i))
+                nc.vector.tensor_tensor(out=y[:], in0=v[:, cols], in1=windows[b % 2][:, cols], op=ALU.subtract)
+                nc.sync.dma_start(out=out[P * b : P * (b + 1), cols], in_=y[:])
+
+        quantize(interleave(nc.vector.tensor_copy, we_first[:], 2 * P, "grouped0", "window1"), 0, 2)
+        windows = []
+        for i in range(2):
+            window = tile([P, T], F32, "window%d" % i)
+            nc.vector.memset(window[:], 0.0)
+            windows.append(window)
+
+        u = shared(0)
+        gain = expert(0)
+        d = gather(0, u, gain)
+        scatter(0, d)
+        r = scaled_residual(0)
+        v = plain_sum(0, u, r)
+        we_rest = tile([P, PACK, 2 * P], F32, "we_rest")
+        nc.sync.dma_start(out=we_rest[:], in_=we_rows[:, :, 2 * P : N])
+        quantize(interleave(nc.scalar.copy, we_rest[:], 2 * P, "grouped2", None), 2, 2)
+        for b in range(1, BLOCKS):
+            gain = expert(b)
+            u = shared(b)
+            r = scaled_residual(b)
+            d = gather(b, u, gain)
+            finish(b - 1, v)
+            scatter(b, d)
+            v = plain_sum(b, u, r)
+        finish(BLOCKS - 1, v)

@@ -1,6 +1,7 @@
 from contextlib import ExitStack
 
 import concourse.mybir as mybir
+from concourse.masks import make_identity
 
 K, L, T, J, N = 1024, 512, 1024, 512, 512
 FLOPS = 2 * K * N * T + 2 * L * N * J
@@ -27,8 +28,7 @@ def tile_moe_expert_scales_shared_answer_kernel(tc, xt_words, xt_scales, ws_word
     nc = tc.nc
     with ExitStack() as ctx:
         held = ctx.enter_context(tc.tile_pool(name="held", bufs=1))
-        psum_u = ctx.enter_context(tc.psum_pool(name="psum_u", bufs=4))
-        psum_p = ctx.enter_context(tc.psum_pool(name="psum_p", bufs=2))
+        psum = ctx.enter_context(tc.psum_pool(name="psum", bufs=1))
 
         def tile(shape, dtype, name, tag=None):
             return held.tile(shape, dtype, name=name, tag=tag or name, align_bytes=64)
@@ -38,10 +38,9 @@ def tile_moe_expert_scales_shared_answer_kernel(tc, xt_words, xt_scales, ws_word
         ws_plane = tile([P, PASSES, N], U8, "ws_plane")
         xe_plane = tile([P, 1, J], U8, "xe_plane")
 
-        def load_plane(queue, plane, scales):
+        def load_scale_row(plane, scales, r):
             rows = scales.rearrange("z (q r) c -> r q z c", r=4)
-            for r in range(4):
-                queue.dma_start(out=plane[r:P:32, :, :].bitcast(I32), in_=rows[r].bitcast(I32))
+            nc.sync.dma_start(out=plane[r:P:32, :, :].bitcast(I32), in_=rows[r].bitcast(I32))
 
         we_rows = we.rearrange("(p j) n -> p j n", j=PACK)
         xt_rows = xt_words.rearrange("z p c r -> p z (c r)")
@@ -51,52 +50,73 @@ def tile_moe_expert_scales_shared_answer_kernel(tc, xt_words, xt_scales, ws_word
             nc.sync.dma_start(out=half[:].bitcast(I32), in_=xt_rows[:, :, 4 * BANK * h : 4 * BANK * (h + 1)].bitcast(I32))
             return half
 
-        load_plane(nc.sync, xt_plane, xt_scales)
-        we_first = tile([P, PACK, 2 * P], F32, "we_first", tag="window0")
-        nc.sync.dma_start(out=we_first[:], in_=we_rows[:, :, 0 : 2 * P])
-        xe_codes = tile([P, J], U32, "xe_codes")
-        nc.sync.dma_start(out=xe_codes[:].bitcast(I32), in_=xe_words[0].rearrange("p c r -> p (c r)").bitcast(I32))
+        for r in (0, 1):
+            load_scale_row(xt_plane, xt_scales, r)
         ws_codes = tile([P, PASSES, 2 * N], U8, "ws_codes")
         nc.sync.dma_start(out=ws_codes[:].bitcast(I32), in_=ws_words.rearrange("z p c -> p z c").bitcast(I32))
+        for r in (2, 3):
+            load_scale_row(xt_plane, xt_scales, r)
+        for r in (0, 1):
+            load_scale_row(ws_plane, ws_scales, r)
         xt_codes = [load_tokens(0)]
-        load_plane(nc.sync, ws_plane, ws_scales)
+        for r in (2, 3):
+            load_scale_row(ws_plane, ws_scales, r)
+        we_first = tile([P, PACK, 2 * P], F32, "we_first")
+        nc.sync.dma_start(out=we_first[:], in_=we_rows[:, :, 0 : 2 * P])
         xt_codes.append(load_tokens(1))
-        load_plane(nc.sync, xe_plane, xe_scales)
         nc.sync.dma_start(offsets[:], offs)
+        xe_codes = tile([P, J], U32, "xe_codes")
+        nc.sync.dma_start(out=xe_codes[:].bitcast(I32), in_=xe_words[0].rearrange("p c r -> p (c r)").bitcast(I32))
+        for r in range(4):
+            load_scale_row(xe_plane, xe_scales, r)
+
+        we_rest = tile([P, PACK, 2 * P], F32, "we_rest")
+        nc.sync.dma_start(out=we_rest[:], in_=we_rows[:, :, 2 * P : N])
+        res_raw = []
+        for b in range(BLOCKS):
+            raw = tile([P, T], F32, "res%d" % b)
+            nc.sync.dma_start(out=raw[:], in_=res[P * b : P * (b + 1), :])
+            res_raw.append(raw)
+
+        identity = tile([P, P], F32, "identity")
+        make_identity(nc, identity[:])
+
+        windows = []
+        for i in range(2):
+            window = tile([P, T], F32, "window%d" % i)
+            nc.vector.memset(window[:], 0.0)
+            windows.append(window)
 
         we_codes = [None] * BLOCKS
         we_plane = [None] * BLOCKS
 
-        def interleave(copy, raw, width, name, tag):
-            grouped = tile([P, width, PACK], BF16, name, tag=tag)
-            copy(
+        def quantize_weights(raw, first):
+            grouped = tile([P, 2 * P, PACK], BF16, "grouped%d" % first)
+            nc.vector.tensor_copy(
                 out=grouped[:].rearrange("p (c i) t -> p c t i", i=4),
-                in_=raw.rearrange("p t (c i) -> p c t i", i=4),
+                in_=raw[:].rearrange("p t (c i) -> p c t i", i=4),
             )
-            return grouped
-
-        def quantize(grouped, first, count):
-            codes = tile([P, count * P], U32, "we_codes%d" % first)
-            plane = tile([P, count * P], U8, "we_plane%d" % first)
+            codes = tile([P, 2 * P], U32, "we_codes%d" % first)
+            plane = tile([P, 2 * P], U8, "we_plane%d" % first)
             nc.vector.quantize_mx(out=codes[:].bitcast(FP8X4), scales=plane[:], in_=grouped[:].rearrange("p w t -> p (w t)"))
-            for i in range(count):
+            for i in range(2):
                 we_codes[first + i] = codes[:, i * P : (i + 1) * P]
                 we_plane[first + i] = plane[:, i * P : (i + 1) * P]
 
         def expert(b):
-            acc = psum_p.tile([P, J], F32, name="p_acc")
+            acc = psum.tile([P, J], F32, name="p_acc%d" % b, tag="bank%d" % (4 + b))
             nc.tensor.matmul_mx(
                 out=acc[:], lhsT=we_codes[b].bitcast(FP8X4), lhsT_scale=we_plane[b],
                 rhs=xe_codes[:].bitcast(FP8X4), rhs_scale=xe_plane[:, 0, :], start=True, stop=True,
             )
-            gain = tile([P, J], F32, "gain%d" % b, tag="v" if b == 0 else None)
-            nc.scalar.activation(out=gain[:], in_=acc[:], func=ACT.Tanh)
+            gain = tile([P, J], F32, "gain%d" % b)
+            nc.scalar.activation(out=gain[:], in_=acc[:], func=ACT.Tanh, scale=-1.0)
             return gain
 
         def shared(b):
             u = tile([P, T], F32, "u%d" % b)
             for h in range(2):
-                acc = psum_u.tile([P, BANK], F32, name="u_acc")
+                acc = psum.tile([P, BANK], F32, name="u_acc%d_%d" % (b, h), tag="bank%d" % (2 * b + h))
                 for z in range(PASSES):
                     nc.tensor.matmul_mx(
                         out=acc[:],
@@ -113,60 +133,69 @@ def tile_moe_expert_scales_shared_answer_kernel(tc, xt_words, xt_scales, ws_word
             return u
 
         def scaled_residual(b):
-            raw = tile([P, T], F32, "res%d" % b, tag="res_raw")
-            nc.sync.dma_start(out=raw[:], in_=res[P * b : P * (b + 1), :])
-            r = tile([P, T], F32, "r%d" % b, tag="r%d" % b)
+            halves = []
             for h in range(2):
-                cols = slice(BANK * h, BANK * (h + 1))
-                nc.scalar.activation(out=r[:, cols], in_=raw[:, cols], func=ACT.Copy, scale=0.2)
-            return r
+                r = tile([P, BANK], F32, "r%d_%d" % (b, h))
+                nc.scalar.activation(out=r[:], in_=res_raw[b][:, BANK * h : BANK * (h + 1)], func=ACT.Copy, scale=0.2)
+                halves.append(r)
+            return halves
 
-        def gather(b, u, gain):
-            d = tile([P, J], F32, "d%d" % b, tag="r%d" % (b - 1) if b else None)
-            nc.vector.tensor_tensor(out=d[:], in0=u[:].indirect(offsets[:]), in1=gain[:], op=ALU.mult)
-            return d
+        def gather_pair(first, u, gains, tag):
+            pair = tile([P, 2, J], F32, "d%d" % first, tag=tag)
+            for i in range(2):
+                nc.vector.tensor_tensor(out=pair[:, i, :], in0=u[first + i][:].indirect(offsets[:]), in1=gains[first + i][:], op=ALU.mult)
+            return [pair[:, 0, :], pair[:, 1, :]]
 
         def scatter(b, d):
-            nc.vector.tensor_copy(out=windows[b % 2][:].indirect(offsets[:]), in_=d[:])
+            nc.vector.tensor_copy(out=windows[b % 2][:].indirect(offsets[:]), in_=d)
 
         def plain_sum(b, u, r):
-            v = tile([P, T], F32, "v%d" % b, tag="v")
+            v = tile([P, T], F32, "v%d" % b, tag="gain%d" % b)
             for h in range(2):
                 cols = slice(BANK * h, BANK * (h + 1))
-                nc.gpsimd.tensor_tensor(out=v[:, cols], in0=u[:, cols], in1=r[:, cols], op=ALU.add)
+                nc.gpsimd.tensor_tensor(out=v[:, cols], in0=u[:, cols], in1=r[h][:], op=ALU.add)
             return v
 
-        def finish(b, v):
-            pieces = 2 if b == BLOCKS - 1 else 1
-            width = T // pieces
-            for i in range(pieces):
-                cols = slice(width * i, width * (i + 1))
-                y = tile([P, width], F32, "y%d_%d" % (b, i))
-                nc.vector.tensor_tensor(out=y[:], in0=v[:, cols], in1=windows[b % 2][:, cols], op=ALU.subtract)
+        def finish_on_tensor(b, v, halves):
+            for h in halves:
+                turned = psum.tile([P, BANK], F32, name="turned%d_%d" % (b, h), tag="bank%d" % h)
+                for c in range(0, BANK, P):
+                    cols = slice(BANK * h + c, BANK * h + c + P)
+                    nc.tensor.matmul(out=turned[:, c : c + P], lhsT=v[:, cols], rhs=identity[:], start=True, stop=False, is_transpose=True)
+                    nc.tensor.matmul(out=turned[:, c : c + P], lhsT=windows[b % 2][:, cols], rhs=identity[:], start=False, stop=True, is_transpose=True)
+                staged = tile([P, BANK], F32, "staged%d_%d" % (b, h), tag="staged%d" % h)
+                nc.scalar.copy(out=staged[:], in_=turned[:])
+                back = psum.tile([P, BANK], F32, name="back%d_%d" % (b, h), tag="bank%d" % (2 + h))
+                for c in range(0, BANK, P):
+                    nc.tensor.transpose(back[:, c : c + P], staged[:, c : c + P], identity[:])
+                y = tile([P, BANK], F32, "y%d_%d" % (b, h))
+                nc.scalar.copy(out=y[:], in_=back[:])
+                nc.sync.dma_start(out=out[P * b : P * (b + 1), BANK * h : BANK * (h + 1)], in_=y[:])
+
+        def finish_by_add(engine, b, v, halves):
+            for h in halves:
+                cols = slice(BANK * h, BANK * (h + 1))
+                y = tile([P, BANK], F32, "y%d_%d" % (b, h))
+                engine.tensor_tensor(out=y[:], in0=v[:, cols], in1=windows[b % 2][:, cols], op=ALU.add)
                 nc.sync.dma_start(out=out[P * b : P * (b + 1), cols], in_=y[:])
 
-        quantize(interleave(nc.vector.tensor_copy, we_first[:], 2 * P, "grouped0", "window1"), 0, 2)
-        windows = []
-        for i in range(2):
-            window = tile([P, T], F32, "window%d" % i)
-            nc.vector.memset(window[:], 0.0)
-            windows.append(window)
-
-        u = shared(0)
-        gain = expert(0)
-        d = gather(0, u, gain)
-        scatter(0, d)
-        r = scaled_residual(0)
-        v = plain_sum(0, u, r)
-        we_rest = tile([P, PACK, 2 * P], F32, "we_rest")
-        nc.sync.dma_start(out=we_rest[:], in_=we_rows[:, :, 2 * P : N])
-        quantize(interleave(nc.scalar.copy, we_rest[:], 2 * P, "grouped2", None), 2, 2)
-        for b in range(1, BLOCKS):
-            gain = expert(b)
-            u = shared(b)
-            r = scaled_residual(b)
-            d = gather(b, u, gain)
-            finish(b - 1, v)
-            scatter(b, d)
-            v = plain_sum(b, u, r)
-        finish(BLOCKS - 1, v)
+        quantize_weights(we_first, 0)
+        u = [shared(0)]
+        gains = [expert(0), expert(1)]
+        u.append(shared(1))
+        quantize_weights(we_rest, 2)
+        d = gather_pair(0, u, gains, None)
+        v = []
+        for b in range(2):
+            scatter(b, d[b])
+            v.append(plain_sum(b, u[b], scaled_residual(b)))
+        gains.extend([expert(2), expert(3)])
+        u.extend([shared(2), shared(3)])
+        d.extend(gather_pair(2, u, gains, "r1_1"))
+        for b in range(2, BLOCKS):
+            finish_on_tensor(b - 2, v[b - 2], (0, 1))
+            scatter(b, d[b])
+            v.append(plain_sum(b, u[b], scaled_residual(b)))
+        finish_on_tensor(2, v[2], (0,))
+        finish_by_add(nc.gpsimd, 2, v[2], (1,))
+        finish_by_add(nc.vector, 3, v[3], (0, 1))

@@ -63,15 +63,14 @@ def tile_moe_expert_scales_shared_answer_kernel(tc, xt_words, xt_scales, ws_word
             load_scale_row(ws_plane, ws_scales, r)
         we_first = tile([P, PACK, 2 * P], F32, "we_first")
         nc.sync.dma_start(out=we_first[:], in_=we_rows[:, :, 0 : 2 * P])
-        xt_codes.append(load_tokens(1))
-        nc.sync.dma_start(offsets[:], offs)
         xe_codes = tile([P, J], U32, "xe_codes")
         nc.sync.dma_start(out=xe_codes[:].bitcast(I32), in_=xe_words[0].rearrange("p c r -> p (c r)").bitcast(I32))
-        for r in range(4):
-            load_scale_row(xe_plane, xe_scales, r)
-
         we_rest = tile([P, PACK, 2 * P], F32, "we_rest")
         nc.sync.dma_start(out=we_rest[:], in_=we_rows[:, :, 2 * P : N])
+        for r in range(4):
+            load_scale_row(xe_plane, xe_scales, r)
+        xt_codes.append(load_tokens(1))
+        nc.sync.dma_start(offsets[:], offs)
         res_raw = []
         for b in range(BLOCKS):
             raw = tile([P, T], F32, "res%d" % b)
@@ -116,7 +115,7 @@ def tile_moe_expert_scales_shared_answer_kernel(tc, xt_words, xt_scales, ws_word
         def shared(b):
             u = tile([P, T], F32, "u%d" % b)
             for h in range(2):
-                acc = psum.tile([P, BANK], F32, name="u_acc%d_%d" % (b, h), tag="bank%d" % (2 * b + h))
+                acc = psum.tile([P, BANK], F32, name="u_acc%d_%d" % (b, h), tag="bank%d" % ((0, 1), (2, 3), (1, 3), (6, 7))[b][h])
                 for z in range(PASSES):
                     nc.tensor.matmul_mx(
                         out=acc[:],
@@ -149,53 +148,55 @@ def tile_moe_expert_scales_shared_answer_kernel(tc, xt_words, xt_scales, ws_word
         def scatter(b, d):
             nc.vector.tensor_copy(out=windows[b % 2][:].indirect(offsets[:]), in_=d)
 
-        def plain_sum(b, u, r):
-            v = tile([P, T], F32, "v%d" % b, tag="gain%d" % b)
+        def plain_sum(b, u):
+            r = scaled_residual(b)
+            halves = []
             for h in range(2):
-                cols = slice(BANK * h, BANK * (h + 1))
-                nc.gpsimd.tensor_tensor(out=v[:, cols], in0=u[:, cols], in1=r[h][:], op=ALU.add)
-            return v
+                v = tile([P, BANK], F32, "v%d_%d" % (b, h), tag=("gain%d" % b, "r%d_0" % b)[h])
+                nc.gpsimd.tensor_tensor(out=v[:], in0=u[:, BANK * h : BANK * (h + 1)], in1=r[h][:], op=ALU.add)
+                halves.append(v)
+            return halves
 
         def finish_on_tensor(b, v, halves):
             for h in halves:
-                turned = psum.tile([P, BANK], F32, name="turned%d_%d" % (b, h), tag="bank%d" % h)
+                turned = psum.tile([P, BANK], F32, name="turned%d_%d" % (b, h), tag="bank%d" % (2 * h))
                 for c in range(0, BANK, P):
                     cols = slice(BANK * h + c, BANK * h + c + P)
-                    nc.tensor.matmul(out=turned[:, c : c + P], lhsT=v[:, cols], rhs=identity[:], start=True, stop=False, is_transpose=True)
+                    nc.tensor.matmul(out=turned[:, c : c + P], lhsT=v[h][:, c : c + P], rhs=identity[:], start=True, stop=False, is_transpose=True)
                     nc.tensor.matmul(out=turned[:, c : c + P], lhsT=windows[b % 2][:, cols], rhs=identity[:], start=False, stop=True, is_transpose=True)
                 staged = tile([P, BANK], F32, "staged%d_%d" % (b, h), tag="staged%d" % h)
                 nc.scalar.copy(out=staged[:], in_=turned[:])
-                back = psum.tile([P, BANK], F32, name="back%d_%d" % (b, h), tag="bank%d" % (2 + h))
+                back = psum.tile([P, BANK], F32, name="back%d_%d" % (b, h), tag="bank%d" % (4 + h))
                 for c in range(0, BANK, P):
                     nc.tensor.transpose(back[:, c : c + P], staged[:, c : c + P], identity[:])
                 y = tile([P, BANK], F32, "y%d_%d" % (b, h))
                 nc.scalar.copy(out=y[:], in_=back[:])
-                nc.sync.dma_start(out=out[P * b : P * (b + 1), BANK * h : BANK * (h + 1)], in_=y[:])
+                nc.scalar.dma_start(out=out[P * b : P * (b + 1), BANK * h : BANK * (h + 1)], in_=y[:])
 
-        def finish_by_add(engine, b, v, halves):
-            for h in halves:
-                cols = slice(BANK * h, BANK * (h + 1))
-                y = tile([P, BANK], F32, "y%d_%d" % (b, h))
-                engine.tensor_tensor(out=y[:], in0=v[:, cols], in1=windows[b % 2][:, cols], op=ALU.add)
-                nc.sync.dma_start(out=out[P * b : P * (b + 1), cols], in_=y[:])
+        def finish_by_add(engine, b, v, y, first, width):
+            h, c = divmod(first, BANK)
+            cols = slice(first, first + width)
+            engine.tensor_tensor(out=y, in0=v[h][:, c : c + width], in1=windows[b % 2][:, cols], op=ALU.add)
+            nc.sync.dma_start(out=out[P * b : P * (b + 1), cols], in_=y)
 
         quantize_weights(we_first, 0)
-        u = [shared(0)]
         gains = [expert(0), expert(1)]
-        u.append(shared(1))
         quantize_weights(we_rest, 2)
+        u = [shared(0), shared(1)]
         d = gather_pair(0, u, gains, None)
-        v = []
-        for b in range(2):
-            scatter(b, d[b])
-            v.append(plain_sum(b, u[b], scaled_residual(b)))
+        scatter(0, d[0])
+        v = [plain_sum(0, u[0])]
         gains.extend([expert(2), expert(3)])
+        scatter(1, d[1])
+        v.append(plain_sum(1, u[1]))
         u.extend([shared(2), shared(3)])
         d.extend(gather_pair(2, u, gains, "r1_1"))
         for b in range(2, BLOCKS):
             finish_on_tensor(b - 2, v[b - 2], (0, 1))
             scatter(b, d[b])
-            v.append(plain_sum(b, u[b], scaled_residual(b)))
+            v.append(plain_sum(b, u[b]))
         finish_on_tensor(2, v[2], (0,))
-        finish_by_add(nc.gpsimd, 2, v[2], (1,))
-        finish_by_add(nc.vector, 3, v[3], (0, 1))
+        finish_by_add(nc.gpsimd, 2, v[2], tile([P, BANK], F32, "y2_late")[:], BANK, BANK)
+        y_last = tile([P, T], F32, "y_last", tag="r2_0")
+        for first, width in ((0, BANK), (BANK, BANK // 2), (BANK + BANK // 2, BANK // 2)):
+            finish_by_add(nc.vector, 3, v[3], y_last[:, first : first + width], first, width)

@@ -61,12 +61,10 @@ def tile_moe_expert_scales_shared_answer_kernel(tc, xt_words, xt_scales, ws_word
         xt_codes = [load_tokens(0)]
         for r in (2, 3):
             load_scale_row(ws_plane, ws_scales, r)
-        we_first = tile([P, PACK, 2 * P], F32, "we_first")
-        nc.sync.dma_start(out=we_first[:], in_=we_rows[:, :, 0 : 2 * P])
+        we_raw = tile([P, PACK, N], F32, "we_raw")
+        nc.sync.dma_start(out=we_raw[:], in_=we_rows)
         xe_codes = tile([P, J], U32, "xe_codes")
         nc.sync.dma_start(out=xe_codes[:].bitcast(I32), in_=xe_words[0].rearrange("p c r -> p (c r)").bitcast(I32))
-        we_rest = tile([P, PACK, 2 * P], F32, "we_rest")
-        nc.sync.dma_start(out=we_rest[:], in_=we_rows[:, :, 2 * P : N])
         for r in range(4):
             load_scale_row(xe_plane, xe_scales, r)
         xt_codes.append(load_tokens(1))
@@ -89,11 +87,11 @@ def tile_moe_expert_scales_shared_answer_kernel(tc, xt_words, xt_scales, ws_word
         we_codes = [None] * BLOCKS
         we_plane = [None] * BLOCKS
 
-        def quantize_weights(raw, first):
+        def quantize_weights(first):
             grouped = tile([P, 2 * P, PACK], BF16, "grouped%d" % first)
             nc.vector.tensor_copy(
                 out=grouped[:].rearrange("p (c i) t -> p c t i", i=4),
-                in_=raw[:].rearrange("p t (c i) -> p c t i", i=4),
+                in_=we_raw[:, :, first * P : (first + 2) * P].rearrange("p t (c i) -> p c t i", i=4),
             )
             codes = tile([P, 2 * P], U32, "we_codes%d" % first)
             plane = tile([P, 2 * P], U8, "we_plane%d" % first)
@@ -148,8 +146,7 @@ def tile_moe_expert_scales_shared_answer_kernel(tc, xt_words, xt_scales, ws_word
         def scatter(b, d):
             nc.vector.tensor_copy(out=windows[b % 2][:].indirect(offsets[:]), in_=d)
 
-        def plain_sum(b, u):
-            r = scaled_residual(b)
+        def plain_sum(b, u, r):
             halves = []
             for h in range(2):
                 v = tile([P, BANK], F32, "v%d_%d" % (b, h), tag=("gain%d" % b, "r%d_0" % b)[h])
@@ -179,22 +176,25 @@ def tile_moe_expert_scales_shared_answer_kernel(tc, xt_words, xt_scales, ws_word
             engine.tensor_tensor(out=y, in0=v[h][:, c : c + width], in1=windows[b % 2][:, cols], op=ALU.add)
             nc.sync.dma_start(out=out[P * b : P * (b + 1), cols], in_=y)
 
-        quantize_weights(we_first, 0)
+        quantize_weights(0)
         gains = [expert(0), expert(1)]
-        quantize_weights(we_rest, 2)
+        quantize_weights(2)
         u = [shared(0), shared(1)]
         d = gather_pair(0, u, gains, None)
         scatter(0, d[0])
-        v = [plain_sum(0, u[0])]
+        r = [scaled_residual(0)]
+        v = [plain_sum(0, u[0], r[0])]
         gains.extend([expert(2), expert(3)])
         scatter(1, d[1])
-        v.append(plain_sum(1, u[1]))
+        r.append(scaled_residual(1))
+        v.append(plain_sum(1, u[1], r[1]))
         u.extend([shared(2), shared(3)])
+        r.extend([scaled_residual(2), scaled_residual(3)])
         d.extend(gather_pair(2, u, gains, "r1_1"))
         for b in range(2, BLOCKS):
             finish_on_tensor(b - 2, v[b - 2], (0, 1))
             scatter(b, d[b])
-            v.append(plain_sum(b, u[b]))
+            v.append(plain_sum(b, u[b], r[b]))
         finish_on_tensor(2, v[2], (0,))
         finish_by_add(nc.gpsimd, 2, v[2], tile([P, BANK], F32, "y2_late")[:], BANK, BANK)
         y_last = tile([P, T], F32, "y_last", tag="r2_0")

from contextlib import ExitStack

import concourse.mybir as mybir
from concourse.masks import make_identity

K, L, T, J, N = 1024, 512, 1024, 512, 512
FLOPS = 2 * K * N * T + 2 * L * N * J

F32 = mybir.dt.float32
BF16 = mybir.dt.bfloat16
I32 = mybir.dt.int32
U32 = mybir.dt.uint32
U16 = mybir.dt.uint16
U8 = mybir.dt.uint8
FP8X4 = mybir.dt.float8_e4m3fn_x4
FP4X4 = mybir.dt.float4_e2m1fn_x4
ACT = mybir.ActivationFunctionType
ALU = mybir.AluOpType

P = 128
PACK = 4
BLOCKS = N // P
BANK = 512
PASSES = K // 512


def tile_moe_expert_scales_shared_answer_kernel(tc, xt_words, xt_scales, ws_words, ws_scales, xe_words, xe_scales, we, res, offs, out):
    nc = tc.nc
    with ExitStack() as ctx:
        held = ctx.enter_context(tc.tile_pool(name="held", bufs=1))
        psum = ctx.enter_context(tc.psum_pool(name="psum", bufs=1))

        def tile(shape, dtype, name, tag=None):
            return held.tile(shape, dtype, name=name, tag=tag or name, align_bytes=64)

        offsets = held.tile([P, J // 16], U16, name="offsets")
        xt_plane = tile([P, PASSES, T], U8, "xt_plane")
        ws_plane = tile([P, PASSES, N], U8, "ws_plane")
        xe_plane = tile([P, 1, J], U8, "xe_plane")

        def load_scale_row(plane, scales, r):
            rows = scales.rearrange("z (q r) c -> r q z c", r=4)
            nc.sync.dma_start(out=plane[r:P:32, :, :].bitcast(I32), in_=rows[r].bitcast(I32))

        we_rows = we.rearrange("(p j) n -> p j n", j=PACK)
        xt_rows = xt_words.rearrange("z p c r -> p z (c r)")

        def load_tokens(h):
            half = tile([P, PASSES, BANK], U32, "xt_codes%d" % h)
            nc.sync.dma_start(out=half[:].bitcast(I32), in_=xt_rows[:, :, 4 * BANK * h : 4 * BANK * (h + 1)].bitcast(I32))
            return half

        for r in (0, 1):
            load_scale_row(xt_plane, xt_scales, r)
        ws_codes = tile([P, PASSES, 2 * N], U8, "ws_codes")
        nc.sync.dma_start(out=ws_codes[:].bitcast(I32), in_=ws_words.rearrange("z p c -> p z c").bitcast(I32))
        for r in (2, 3):
            load_scale_row(xt_plane, xt_scales, r)
        for r in (0, 1):
            load_scale_row(ws_plane, ws_scales, r)
        xt_codes = [load_tokens(0)]
        for r in (2, 3):
            load_scale_row(ws_plane, ws_scales, r)
        we_raw = tile([P, PACK, N], F32, "we_raw")
        nc.sync.dma_start(out=we_raw[:], in_=we_rows)
        xe_codes = tile([P, J], U32, "xe_codes")
        nc.sync.dma_start(out=xe_codes[:].bitcast(I32), in_=xe_words[0].rearrange("p c r -> p (c r)").bitcast(I32))
        for r in range(4):
            load_scale_row(xe_plane, xe_scales, r)
        xt_codes.append(load_tokens(1))
        nc.sync.dma_start(offsets[:], offs)
        res_raw = []
        for b in range(BLOCKS):
            raw = tile([P, T], F32, "res%d" % b)
            nc.sync.dma_start(out=raw[:], in_=res[P * b : P * (b + 1), :])
            res_raw.append(raw)

        identity = tile([P, P], F32, "identity")
        make_identity(nc, identity[:])

        windows = []
        for i in range(2):
            window = tile([P, T], F32, "window%d" % i)
            nc.vector.memset(window[:], 0.0)
            windows.append(window)

        we_codes = [None] * BLOCKS
        we_plane = [None] * BLOCKS

        def quantize_weights(first):
            grouped = tile([P, 2 * P, PACK], BF16, "grouped%d" % first)
            nc.vector.tensor_copy(
                out=grouped[:].rearrange("p (c i) t -> p c t i", i=4),
                in_=we_raw[:, :, first * P : (first + 2) * P].rearrange("p t (c i) -> p c t i", i=4),
            )
            codes = tile([P, 2 * P], U32, "we_codes%d" % first)
            plane = tile([P, 2 * P], U8, "we_plane%d" % first)
            nc.vector.quantize_mx(out=codes[:].bitcast(FP8X4), scales=plane[:], in_=grouped[:].rearrange("p w t -> p (w t)"))
            for i in range(2):
                we_codes[first + i] = codes[:, i * P : (i + 1) * P]
                we_plane[first + i] = plane[:, i * P : (i + 1) * P]

        def expert(b):
            acc = psum.tile([P, J], F32, name="p_acc%d" % b, tag="bank%d" % (4 + b))
            nc.tensor.matmul_mx(
                out=acc[:], lhsT=we_codes[b].bitcast(FP8X4), lhsT_scale=we_plane[b],
                rhs=xe_codes[:].bitcast(FP8X4), rhs_scale=xe_plane[:, 0, :], start=True, stop=True,
            )
            gain = tile([P, J], F32, "gain%d" % b)
            nc.scalar.activation(out=gain[:], in_=acc[:], func=ACT.Tanh, scale=-1.0)
            return gain

        def shared(b):
            u = tile([P, T], F32, "u%d" % b)
            for h in range(2):
                acc = psum.tile([P, BANK], F32, name="u_acc%d_%d" % (b, h), tag="bank%d" % ((0, 1), (2, 3), (1, 3), (6, 7))[b][h])
                for z in range(PASSES):
                    nc.tensor.matmul_mx(
                        out=acc[:],
                        lhsT=ws_codes[:, z, 2 * P * b : 2 * P * (b + 1)].bitcast(FP4X4),
                        lhsT_scale=ws_plane[:, z, P * b : P * (b + 1)],
                        rhs=xt_codes[h][:, z, :].bitcast(FP8X4),
                        rhs_scale=xt_plane[:, z, BANK * h : BANK * (h + 1)],
                        start=(z == 0), stop=(z == PASSES - 1),
                    )
                if b == 0 and h == 1:
                    nc.vector.tensor_copy(out=u[:, BANK * h : BANK * (h + 1)], in_=acc[:])
                else:
                    nc.scalar.copy(out=u[:, BANK * h : BANK * (h + 1)], in_=acc[:])
            return u

        def scaled_residual(b):
            halves = []
            for h in range(2):
                r = tile([P, BANK], F32, "r%d_%d" % (b, h))
                nc.scalar.activation(out=r[:], in_=res_raw[b][:, BANK * h : BANK * (h + 1)], func=ACT.Copy, scale=0.2)
                halves.append(r)
            return halves

        def gather_pair(first, u, gains, tag):
            pair = tile([P, 2, J], F32, "d%d" % first, tag=tag)
            for i in range(2):
                nc.vector.tensor_tensor(out=pair[:, i, :], in0=u[first + i][:].indirect(offsets[:]), in1=gains[first + i][:], op=ALU.mult)
            return [pair[:, 0, :], pair[:, 1, :]]

        def scatter(b, d):
            nc.vector.tensor_copy(out=windows[b % 2][:].indirect(offsets[:]), in_=d)

        def plain_sum(b, u, r):
            halves = []
            for h in range(2):
                v = tile([P, BANK], F32, "v%d_%d" % (b, h), tag=("gain%d" % b, "r%d_0" % b)[h])
                nc.gpsimd.tensor_tensor(out=v[:], in0=u[:, BANK * h : BANK * (h + 1)], in1=r[h][:], op=ALU.add)
                halves.append(v)
            return halves

        def finish_on_tensor(b, v, halves):
            for h in halves:
                turned = psum.tile([P, BANK], F32, name="turned%d_%d" % (b, h), tag="bank%d" % (2 * h))
                for c in range(0, BANK, P):
                    cols = slice(BANK * h + c, BANK * h + c + P)
                    nc.tensor.matmul(out=turned[:, c : c + P], lhsT=v[h][:, c : c + P], rhs=identity[:], start=True, stop=False, is_transpose=True)
                    nc.tensor.matmul(out=turned[:, c : c + P], lhsT=windows[b % 2][:, cols], rhs=identity[:], start=False, stop=True, is_transpose=True)
                staged = tile([P, BANK], F32, "staged%d_%d" % (b, h), tag="staged%d" % h)
                nc.scalar.copy(out=staged[:], in_=turned[:])
                back = psum.tile([P, BANK], F32, name="back%d_%d" % (b, h), tag="bank%d" % (4 + h))
                for c in range(0, BANK, P):
                    nc.tensor.transpose(back[:, c : c + P], staged[:, c : c + P], identity[:])
                y = tile([P, BANK], F32, "y%d_%d" % (b, h))
                nc.scalar.copy(out=y[:], in_=back[:])
                nc.scalar.dma_start(out=out[P * b : P * (b + 1), BANK * h : BANK * (h + 1)], in_=y[:])

        def finish_by_add(engine, b, v, y, first, width):
            h, c = divmod(first, BANK)
            cols = slice(first, first + width)
            engine.tensor_tensor(out=y, in0=v[h][:, c : c + width], in1=windows[b % 2][:, cols], op=ALU.add)
            nc.sync.dma_start(out=out[P * b : P * (b + 1), cols], in_=y)

        quantize_weights(0)
        gains = [expert(0), expert(1)]
        quantize_weights(2)
        u = [shared(0), shared(1)]
        d = gather_pair(0, u, gains, None)
        scatter(0, d[0])
        r = [scaled_residual(0)]
        v = [plain_sum(0, u[0], r[0])]
        gains.extend([expert(2), expert(3)])
        scatter(1, d[1])
        r.append(scaled_residual(1))
        v.append(plain_sum(1, u[1], r[1]))
        u.extend([shared(2), shared(3)])
        r.extend([scaled_residual(2), scaled_residual(3)])
        d.extend(gather_pair(2, u, gains, "r1_1"))
        for b in range(2, BLOCKS):
            finish_on_tensor(b - 2, v[b - 2], (0, 1))
            scatter(b, d[b])
            v.append(plain_sum(b, u[b], r[b]))
        finish_on_tensor(2, v[2], (0,))
        finish_by_add(nc.gpsimd, 2, v[2], tile([P, BANK], F32, "y2_late")[:], BANK, BANK)
        y_last = tile([P, T], F32, "y_last", tag="r2_0")
        for first, width in ((0, BANK), (BANK, BANK // 2), (BANK + BANK // 2, BANK // 2)):
            finish_by_add(nc.vector, 3, v[3], y_last[:, first : first + width], first, width)
